import numpy as np
import ml_dtypes


def mxq(x, axis, fmt="e4m3"):
    dtype, down = {"e4m3": (ml_dtypes.float8_e4m3fn, 7), "e5m2": (ml_dtypes.float8_e5m2, 14)}[fmt]
    v = np.moveaxis(np.asarray(x, np.float32).astype(ml_dtypes.bfloat16).astype(np.float64), axis, -1)
    blocks = v.reshape(v.shape[:-1] + (-1, 32))
    amax = np.abs(blocks).max(-1, keepdims=True)
    byte = np.maximum(np.where(amax > 0, np.frexp(amax)[1] - 1 + 127, 0) - down, 1)
    scale = np.exp2(byte - 127.0)
    codes = (blocks / scale).astype(np.float32).astype(dtype).astype(np.float64)
    return np.moveaxis((codes * scale).reshape(v.shape), -1, axis)


WIDE = False


def mx_kscale(k):
    if not WIDE:
        return np.ones(k)
    levels = np.array([10, -10, 5, -5, 0])
    if k % 512:
        return np.exp2(np.random.permutation(np.resize(levels, k // 32))).repeat(32)
    a = np.empty((k // 512, 16))
    for p in range(k // 512):
        a[p, :8] = np.random.permutation(np.resize(levels, 8))
        for g in range(8):
            far = levels[np.abs(levels - a[p, g]) >= 10]
            a[p, g + 8] = far[np.random.randint(len(far))]
    return np.exp2(a.ravel()).repeat(32)


def f64(x):
    return np.asarray(x).astype(np.float64)


def striped(idx):
    return np.tile(idx.reshape(-1, 16).T, (8, 1)).astype(np.uint16)


def unstriped(offs):
    return offs[:16].T.reshape(-1).astype(np.int64)


E2M1 = np.array([0.0, 0.5, 1.0, 1.5, 2.0, 3.0, 4.0, 6.0, -0.0, -0.5, -1.0, -1.5, -2.0, -3.0, -4.0, -6.0])


def pack_weight(w, fmt):
    k, n = w.shape
    w = f64(np.asarray(w, np.float32).astype(ml_dtypes.bfloat16)).reshape(k // 32, 32, n)
    amax = np.abs(w).max(1)
    if fmt == "e4m3":
        byte = np.frexp(amax)[1] - 1 + 127 - 7
    else:
        mant, ex = np.frexp(amax / 6.0)
        byte = np.where(mant > 0.5, ex, ex - 1) + 127
    byte = np.clip(np.where(amax > 0, byte, 1), 1, 254)
    scaled = (w * np.exp2(127.0 - byte)[:, None, :]).reshape(k, n).astype(np.float32)
    by_word = np.ascontiguousarray(scaled.reshape(k // 512, 128, 4, n).transpose(0, 1, 3, 2))
    if fmt == "e4m3":
        words = by_word.astype(ml_dtypes.float8_e4m3fn).view(np.uint8)
    else:
        c = by_word.astype(ml_dtypes.float4_e2m1fn).view(np.uint8) & 0xF
        words = (c[..., 0::2] | (c[..., 1::2] << 4)).reshape(k // 512, 128, 2 * n)
    return np.ascontiguousarray(words), np.ascontiguousarray(byte.astype(np.uint8).reshape(k // 512, 16, n))


def unpack_weight(words, scales, fmt):
    g, _, n = scales.shape
    words = np.ascontiguousarray(words).reshape(g, 128, n, -1)
    if fmt == "e4m3":
        vals = words.view(ml_dtypes.float8_e4m3fn).astype(np.float64)
    else:
        nib = np.empty((g, 128, n, 4), np.uint8)
        nib[..., 0::2] = words & 0xF
        nib[..., 1::2] = words >> 4
        vals = E2M1[nib]
    vals = vals * np.repeat(np.exp2(scales.astype(np.float64) - 127.0), 8, axis=1)[..., None]
    return vals.transpose(0, 1, 3, 2).reshape(g * 512, n)


def silu(v):
    return v / (1.0 + np.exp(-np.maximum(v, -700.0)))


G, K, M, T, S = 2, 512, 256, 2048, 512


def setup_inputs():
    n = np.random.standard_normal
    s = mx_kscale(K)[:, None]
    p_w4 = pack_weight(n((K, M)) / np.sqrt(K) / s, "e2m1")
    p_w8 = pack_weight(n((K, M)) / np.sqrt(K) / s, "e4m3")
    return {
        "xT": (n((K, T)) * s).astype(np.float32),
        "c": (n((K, S)) * s).astype(np.float32),
        "w4_words": p_w4[0],
        "w4_scales": p_w4[1],
        "w8_words": p_w8[0],
        "w8_scales": p_w8[1],
        "b": (0.3 * n(256)).astype(np.float32),
        "offs": striped(np.concatenate([np.random.permutation(T)[:S] for _ in range(G)])),
    }


def reference(xT, c, w4_words, w4_scales, w8_words, w8_scales, b, offs):
    idx = unstriped(offs).reshape(G, S)
    d_ = [mxq(f64(xT)[:, idx[g]] - f64(c), 0, "e4m3") for g in range(G)]
    c_ = mxq(f64(c), 0, "e4m3")
    w4_ = unpack_weight(w4_words, w4_scales, "e2m1")
    w8_ = unpack_weight(w8_words, w8_scales, "e4m3")
    y = np.max([(w4_.T @ d) for d in d_], axis=0) + (w8_.T @ c_)
    return silu(y + f64(b)[:, None])

@@ -1,0 +1,157 @@
+from contextlib import ExitStack
+
+import concourse.mybir as mybir
+
+G, K, M, T, S = 2, 512, 256, 2048, 512
+FLOPS = 2 * K * M * S * (G + 1)
+
+F32 = mybir.dt.float32
+BF16 = mybir.dt.bfloat16
+I32 = mybir.dt.int32
+U32 = mybir.dt.uint32
+U16 = mybir.dt.uint16
+U8 = mybir.dt.uint8
+FP8X4 = mybir.dt.float8_e4m3fn_x4
+FP4X4 = mybir.dt.float4_e2m1fn_x4
+ALU = mybir.AluOpType
+ACT = mybir.ActivationFunctionType
+
+P = 128
+PACK = 4
+HALVES = M // P
+PER_COL = 16
+CHUNKS = ((0, 256), (256, 128), (384, 128))
+
+
+def tile_list_edge_silu_kernel(tc, xT, c, w4_words, w4_scales, w8_words, w8_scales, b, offs, out):
+    nc = tc.nc
+    with ExitStack() as ctx:
+        keep = ctx.enter_context(tc.tile_pool(name="keep", bufs=1))
+        psum = ctx.enter_context(tc.psum_pool(name="psum", bufs=1))
+
+        offsets = keep.tile([P, G * S // PER_COL], U16, name="offsets")
+        planes = [keep.tile([P, T], F32, name="plane%d" % t) for t in range(PACK)]
+        c_raw = keep.tile([P, PACK, S], F32, name="c_raw")
+        w4 = keep.tile([P, 2 * M], U8, name="w4", align_bytes=64)
+        w4_sc = keep.tile([P, M], U8, name="w4_sc", align_bytes=64)
+        w8 = keep.tile([P, M], U32, name="w8", align_bytes=64)
+        w8_sc = keep.tile([P, M], U8, name="w8_sc", align_bytes=64)
+        bias = keep.tile([P, HALVES], F32, name="bias")
+        warm = keep.tile([P, 2], F32, name="warm")
+
+        x_rows = xT.rearrange("(p t) n -> t p n", t=PACK)
+        c_rows = c.rearrange("(p t) j -> p t j", t=PACK)
+        out_rows = out.rearrange("(h p) j -> p h j", p=P)
+
+        nc.vector.memset(w8_sc[:].bitcast(U32), 0)
+        nc.vector.memset(w4_sc[:].bitcast(U32), 0)
+        nc.vector.memset(warm[:, 0:1], 0.0)
+
+        nc.sync.dma_start(planes[0][:], x_rows[0])
+        nc.sync.dma_start(offsets[:], offs)
+        nc.sync.dma_start(c_raw[:, 0, :], c_rows[:, 0, :])
+        nc.sync.dma_start(c_raw[:, 1:PACK, :], c_rows[:, 1:PACK, :])
+        for t in range(1, PACK):
+            nc.sync.dma_start(planes[t][:], x_rows[t])
+
+        def load_scales(queue, tile, src):
+            for q in range(4):
+                queue.dma_start(tile[32 * q : 32 * q + 4, :].bitcast(I32), src[0, 4 * q : 4 * q + 4, :].bitcast(I32))
+
+        nc.scalar.dma_start(w8[:].bitcast(I32), w8_words[0].rearrange("p n t -> p (n t)").bitcast(I32))
+        with nc.allow_non_contiguous_dma(reason="one bias value a partition"):
+            nc.scalar.dma_start(bias[:], b.rearrange("(h p) -> p h", p=P))
+        load_scales(nc.scalar, w8_sc, w8_scales)
+        nc.scalar.activation(warm[:, 1:2], warm[:, 0:1], ACT.Silu)
+
+        nc.sync.dma_start(w4[:].bitcast(I32), w4_words[0].bitcast(I32))
+        load_scales(nc.sync, w4_sc, w4_scales)
+
+        diff = [[keep.tile([P, 2, S], F32, name="diff%d_%d" % (g, u)) for u in range(2)] for g in range(G)]
+
+        def gather(g, t, j0, n):
+            cols = slice((g * S + j0) // PER_COL, (g * S + j0 + n) // PER_COL)
+            nc.vector.tensor_tensor(
+                diff[g][t // 2][:, t % 2, j0 : j0 + n],
+                planes[t][:].indirect(offsets[:, cols]),
+                c_raw[:, t, j0 : j0 + n],
+                ALU.subtract,
+            )
+
+        woven = {}
+        for g in range(G):
+            for j0, n in CHUNKS:
+                woven[g, j0] = keep.tile([P, n, PACK], BF16, name="woven%d_%d" % (g, j0), align_bytes=64)
+
+        def weave(copy, g, u, j0, n):
+            copy(woven[g, j0][:, :, 2 * u : 2 * u + 2], diff[g][u][:, :, j0 : j0 + n].rearrange("p t j -> p j t"))
+
+        def quantize(name, src, n):
+            codes = keep.tile([P, n], U32, name=name + "_codes", align_bytes=64)
+            scales = keep.tile([P, n], U8, name=name + "_scales", align_bytes=64)
+            nc.vector.quantize_mx(out=codes[:].bitcast(FP8X4), scales=scales[:], in_=src.rearrange("p j t -> p (j t)"))
+            return codes, scales
+
+        for g in range(G):
+            gather(g, 0, 0, S)
+
+        c_woven = [keep.tile([P, S // 2, PACK], BF16, name="c_woven%d" % i, align_bytes=64) for i in range(2)]
+        own = keep.tile([P, HALVES, S], F32, name="own")
+        for i, copy in enumerate((nc.scalar.copy, nc.vector.tensor_copy)):
+            j0, n = i * S // 2, S // 2
+            copy(c_woven[i][:].rearrange("p (a i) t -> p a t i", i=4), c_raw[:, :, j0 : j0 + n].rearrange("p t (a i) -> p a t i", i=4))
+        for i in range(2):
+            j0, n = i * S // 2, S // 2
+            codes, scales = quantize("c%d" % i, c_woven[i][:], n)
+            acc = psum.tile([P, HALVES, n], F32, name="own_acc%d" % i)
+            for h in range(HALVES):
+                nc.tensor.matmul_mx(
+                    out=acc[:, h, :],
+                    lhsT=w8[:, h * P : (h + 1) * P].bitcast(FP8X4),
+                    lhsT_scale=w8_sc[:, h * P : (h + 1) * P],
+                    rhs=codes[:].bitcast(FP8X4),
+                    rhs_scale=scales[:],
+                    start=True,
+                    stop=True,
+                )
+            for h in range(HALVES):
+                nc.scalar.activation(own[:, h, j0 : j0 + n], acc[:, h, :], ACT.Identity, bias=bias[:, h : h + 1])
+
+        for g in range(G):
+            gather(g, 1, 0, S)
+            for j0, n in CHUNKS:
+                weave(nc.scalar.copy, g, 0, j0, n)
+        for g in range(G):
+            gather(g, 2, 0, S)
+
+        def project(g, j0, n):
+            codes, scales = quantize("d%d_%d" % (g, j0), woven[g, j0][:], n)
+            acc = psum.tile([P, HALVES, n], F32, name="acc%d_%d" % (g, j0))
+            for h in range(HALVES):
+                nc.tensor.matmul_mx(
+                    out=acc[:, h, :],
+                    lhsT=w4[:, 2 * h * P : 2 * (h + 1) * P].bitcast(FP4X4),
+                    lhsT_scale=w4_sc[:, h * P : (h + 1) * P],
+                    rhs=codes[:].bitcast(FP8X4),
+                    rhs_scale=scales[:],
+                    start=True,
+                    stop=True,
+                )
+            return acc
+
+        for j0, n in CHUNKS:
+            for g in range(G):
+                gather(g, 3, j0, n)
+                weave(nc.scalar.copy, g, 1, j0, n)
+        for j0, n in CHUNKS:
+            acc0 = project(0, j0, n)
+            first = keep.tile([P, HALVES, n], F32, name="first%d" % j0)
+            nc.scalar.copy(first[:], acc0[:])
+            acc1 = project(1, j0, n)
+            best = keep.tile([P, HALVES, n], F32, name="best%d" % j0)
+            nc.vector.tensor_tensor(best[:], acc1[:], first[:], ALU.max)
+            total = keep.tile([P, HALVES, n], F32, name="total%d" % j0)
+            nc.vector.tensor_tensor(total[:], best[:], own[:, :, j0 : j0 + n], ALU.add)
+            result = keep.tile([P, HALVES, n], F32, name="result%d" % j0)
+            nc.scalar.activation(result[:], total[:], ACT.Silu)
+            nc.sync.dma_start(out_rows[:, :, j0 : j0 + n], result[:])

@@ -1,6 +1,7 @@
 from contextlib import ExitStack
 
 import concourse.mybir as mybir
+from concourse.masks import make_identity
 
 G, K, M, T, S = 2, 512, 256, 2048, 512
 FLOPS = 2 * K * M * S * (G + 1)
@@ -20,7 +21,9 @@ P = 128
 PACK = 4
 HALVES = M // P
 PER_COL = 16
-CHUNKS = ((0, 256), (256, 128), (384, 128))
+NODES = 128
+CHUNKS = S // NODES
+LAST = CHUNKS - 1
 
 
 def tile_list_edge_silu_kernel(tc, xT, c, w4_words, w4_scales, w8_words, w8_scales, b, offs, out):
@@ -36,38 +39,73 @@ def tile_list_edge_silu_kernel(tc, xT, c, w4_words, w4_scales, w8_words, w8_scal
         w4_sc = keep.tile([P, M], U8, name="w4_sc", align_bytes=64)
         w8 = keep.tile([P, M], U32, name="w8", align_bytes=64)
         w8_sc = keep.tile([P, M], U8, name="w8_sc", align_bytes=64)
+        bias_rows = keep.tile([P, P], F32, name="bias_rows")
         bias = keep.tile([P, HALVES], F32, name="bias")
         warm = keep.tile([P, 2], F32, name="warm")
+        ident = keep.tile([P, P], F32, name="ident")
 
         x_rows = xT.rearrange("(p t) n -> t p n", t=PACK)
         c_rows = c.rearrange("(p t) j -> p t j", t=PACK)
         out_rows = out.rearrange("(h p) j -> p h j", p=P)
 
-        nc.vector.memset(w8_sc[:].bitcast(U32), 0)
-        nc.vector.memset(w4_sc[:].bitcast(U32), 0)
-        nc.vector.memset(warm[:, 0:1], 0.0)
-
-        nc.sync.dma_start(planes[0][:], x_rows[0])
-        nc.sync.dma_start(offsets[:], offs)
-        nc.sync.dma_start(c_raw[:, 0, :], c_rows[:, 0, :])
-        nc.sync.dma_start(c_raw[:, 1:PACK, :], c_rows[:, 1:PACK, :])
-        for t in range(1, PACK):
-            nc.sync.dma_start(planes[t][:], x_rows[t])
-
         def load_scales(queue, tile, src):
             for q in range(4):
                 queue.dma_start(tile[32 * q : 32 * q + 4, :].bitcast(I32), src[0, 4 * q : 4 * q + 4, :].bitcast(I32))
 
-        nc.scalar.dma_start(w8[:].bitcast(I32), w8_words[0].rearrange("p n t -> p (n t)").bitcast(I32))
-        with nc.allow_non_contiguous_dma(reason="one bias value a partition"):
-            nc.scalar.dma_start(bias[:], b.rearrange("(h p) -> p h", p=P))
-        load_scales(nc.scalar, w8_sc, w8_scales)
+        nc.vector.memset(w8_sc[:].bitcast(U32), 0)
+        nc.vector.memset(w4_sc[:].bitcast(U32), 0)
+        nc.vector.memset(warm[:, 0:1], 0.0)
         nc.scalar.activation(warm[:, 1:2], warm[:, 0:1], ACT.Silu)
+        nc.gpsimd.memset(bias_rows[:], 0.0)
+        nc.gpsimd.dma_start(bias_rows[0:HALVES, :], b.rearrange("(h p) -> h p", p=P))
+        make_identity(nc, ident[:])
 
+        nc.sync.dma_start(c_raw[:], c_rows)
+        nc.sync.dma_start(planes[0][:], x_rows[0])
+        nc.sync.dma_start(offsets[:], offs)
+        load_scales(nc.sync, w8_sc, w8_scales)
+        nc.sync.dma_start(w8[:].bitcast(I32), w8_words[0].rearrange("p n t -> p (n t)").bitcast(I32))
+        for t in range(1, PACK):
+            nc.sync.dma_start(planes[t][:], x_rows[t])
         nc.sync.dma_start(w4[:].bitcast(I32), w4_words[0].bitcast(I32))
         load_scales(nc.sync, w4_sc, w4_scales)
 
+        def quantize(name, src, n):
+            codes = keep.tile([P, n], U32, name=name + "_codes", align_bytes=64)
+            scales = keep.tile([P, n], U8, name=name + "_scales", align_bytes=64)
+            nc.vector.quantize_mx(out=codes[:].bitcast(FP8X4), scales=scales[:], in_=src.rearrange("p j t -> p (j t)"))
+            return codes, scales
+
+        half = S // 2
+        c_woven = [keep.tile([P, half, PACK], BF16, name="c_woven%d" % i, align_bytes=64) for i in range(2)]
+        for i, copy in enumerate((nc.scalar.copy, nc.vector.tensor_copy)):
+            copy(
+                c_woven[i][:].rearrange("p (a i) t -> p a t i", i=4),
+                c_raw[:, :, i * half : (i + 1) * half].rearrange("p t (a i) -> p a t i", i=4),
+            )
+        bias_acc = psum.tile([P, P], F32, name="bias_acc", tag="bank0")
+        nc.tensor.transpose(bias_acc[:], bias_rows[:], ident[:])
+        nc.vector.tensor_copy(bias[:], bias_acc[:, 0:HALVES])
+
+        own = keep.tile([P, HALVES, S], F32, name="own")
+        for i in range(2):
+            codes, scales = quantize("c%d" % i, c_woven[i][:], half)
+            own_acc = psum.tile([P, HALVES, half], F32, name="own_acc%d" % i, tag="bank%d" % (6 + i))
+            for h in range(HALVES):
+                nc.tensor.matmul_mx(
+                    out=own_acc[:, h, :],
+                    lhsT=w8[:, h * P : (h + 1) * P].bitcast(FP8X4),
+                    lhsT_scale=w8_sc[:, h * P : (h + 1) * P],
+                    rhs=codes[:].bitcast(FP8X4),
+                    rhs_scale=scales[:],
+                    start=True,
+                    stop=True,
+                )
+            for h in range(HALVES):
+                nc.scalar.activation(own[:, h, i * half : (i + 1) * half], own_acc[:, h, :], ACT.Identity, bias=bias[:, h : h + 1])
+
         diff = [[keep.tile([P, 2, S], F32, name="diff%d_%d" % (g, u)) for u in range(2)] for g in range(G)]
+        woven = [keep.tile([P, S, PACK], BF16, name="woven%d" % g, align_bytes=64) for g in range(G)]
 
         def gather(g, t, j0, n):
             cols = slice((g * S + j0) // PER_COL, (g * S + j0 + n) // PER_COL)
@@ -78,55 +116,27 @@ def tile_list_edge_silu_kernel(tc, xT, c, w4_words, w4_scales, w8_words, w8_scal
                 ALU.subtract,
             )
 
-        woven = {}
-        for g in range(G):
-            for j0, n in CHUNKS:
-                woven[g, j0] = keep.tile([P, n, PACK], BF16, name="woven%d_%d" % (g, j0), align_bytes=64)
-
         def weave(copy, g, u, j0, n):
-            copy(woven[g, j0][:, :, 2 * u : 2 * u + 2], diff[g][u][:, :, j0 : j0 + n].rearrange("p t j -> p j t"))
-
-        def quantize(name, src, n):
-            codes = keep.tile([P, n], U32, name=name + "_codes", align_bytes=64)
-            scales = keep.tile([P, n], U8, name=name + "_scales", align_bytes=64)
-            nc.vector.quantize_mx(out=codes[:].bitcast(FP8X4), scales=scales[:], in_=src.rearrange("p j t -> p (j t)"))
-            return codes, scales
+            copy(woven[g][:, j0 : j0 + n, 2 * u : 2 * u + 2], diff[g][u][:, :, j0 : j0 + n].rearrange("p t j -> p j t"))
 
         for g in range(G):
             gather(g, 0, 0, S)
-
-        c_woven = [keep.tile([P, S // 2, PACK], BF16, name="c_woven%d" % i, align_bytes=64) for i in range(2)]
-        own = keep.tile([P, HALVES, S], F32, name="own")
-        for i, copy in enumerate((nc.scalar.copy, nc.vector.tensor_copy)):
-            j0, n = i * S // 2, S // 2
-            copy(c_woven[i][:].rearrange("p (a i) t -> p a t i", i=4), c_raw[:, :, j0 : j0 + n].rearrange("p t (a i) -> p a t i", i=4))
-        for i in range(2):
-            j0, n = i * S // 2, S // 2
-            codes, scales = quantize("c%d" % i, c_woven[i][:], n)
-            acc = psum.tile([P, HALVES, n], F32, name="own_acc%d" % i)
-            for h in range(HALVES):
-                nc.tensor.matmul_mx(
-                    out=acc[:, h, :],
-                    lhsT=w8[:, h * P : (h + 1) * P].bitcast(FP8X4),
-                    lhsT_scale=w8_sc[:, h * P : (h + 1) * P],
-                    rhs=codes[:].bitcast(FP8X4),
-                    rhs_scale=scales[:],
-                    start=True,
-                    stop=True,
-                )
-            for h in range(HALVES):
-                nc.scalar.activation(own[:, h, j0 : j0 + n], acc[:, h, :], ACT.Identity, bias=bias[:, h : h + 1])
-
         for g in range(G):
             gather(g, 1, 0, S)
-            for j0, n in CHUNKS:
-                weave(nc.scalar.copy, g, 0, j0, n)
+            weave(nc.scalar.copy, g, 0, 0, S)
         for g in range(G):
             gather(g, 2, 0, S)
 
-        def project(g, j0, n):
-            codes, scales = quantize("d%d_%d" % (g, j0), woven[g, j0][:], n)
-            acc = psum.tile([P, HALVES, n], F32, name="acc%d_%d" % (g, j0))
+        products, firsts, bests = {}, {}, {}
+
+        def bring(k):
+            for g in range(G):
+                gather(g, 3, k * NODES, NODES)
+                weave(nc.vector.tensor_copy if (g, k) in ((1, LAST),) else nc.scalar.copy, g, 1, k * NODES, NODES)
+
+        def project(g, k):
+            codes, scales = quantize("d%d_%d" % (g, k), woven[g][:, k * NODES : (k + 1) * NODES, :], NODES)
+            acc = psum.tile([P, HALVES, NODES], F32, name="acc%d_%d" % (g, k), tag="bank%d" % (G * k + g))
             for h in range(HALVES):
                 nc.tensor.matmul_mx(
                     out=acc[:, h, :],
@@ -137,21 +147,29 @@ def tile_list_edge_silu_kernel(tc, xT, c, w4_words, w4_scales, w8_words, w8_scal
                     start=True,
                     stop=True,
                 )
-            return acc
+            products[g, k] = acc
+            if g == 0:
+                firsts[k] = keep.tile([P, HALVES, NODES], F32, name="first%d" % k)
+                nc.scalar.copy(firsts[k][:], acc[:])
 
-        for j0, n in CHUNKS:
-            for g in range(G):
-                gather(g, 3, j0, n)
-                weave(nc.scalar.copy, g, 1, j0, n)
-        for j0, n in CHUNKS:
-            acc0 = project(0, j0, n)
-            first = keep.tile([P, HALVES, n], F32, name="first%d" % j0)
-            nc.scalar.copy(first[:], acc0[:])
-            acc1 = project(1, j0, n)
-            best = keep.tile([P, HALVES, n], F32, name="best%d" % j0)
-            nc.vector.tensor_tensor(best[:], acc1[:], first[:], ALU.max)
-            total = keep.tile([P, HALVES, n], F32, name="total%d" % j0)
-            nc.vector.tensor_tensor(total[:], best[:], own[:, :, j0 : j0 + n], ALU.add)
-            result = keep.tile([P, HALVES, n], F32, name="result%d" % j0)
+        def choose(k):
+            bests[k] = keep.tile([P, HALVES, NODES], F32, name="best%d" % k)
+            nc.vector.tensor_tensor(bests[k][:], products[1, k][:], firsts[k][:], ALU.max)
+
+        def finish(k):
+            j0 = k * NODES
+            total = keep.tile([P, HALVES, NODES], F32, name="total%d" % k)
+            nc.vector.tensor_tensor(total[:], bests[k][:], own[:, :, j0 : j0 + NODES], ALU.add)
+            result = keep.tile([P, HALVES, NODES], F32, name="result%d" % k)
             nc.scalar.activation(result[:], total[:], ACT.Silu)
-            nc.sync.dma_start(out_rows[:, :, j0 : j0 + n], result[:])
+            nc.sync.dma_start(out_rows[:, :, j0 : j0 + NODES], result[:])
+
+        for k in range(CHUNKS):
+            bring(k)
+            for g in range(G):
+                project(g, k)
+        choose(0)
+        for k in range(CHUNKS):
+            if k < LAST:
+                choose(k + 1)
+            finish(k)

from contextlib import ExitStack

import concourse.mybir as mybir
from concourse.masks import make_identity

G, K, M, T, S = 2, 512, 256, 2048, 512
FLOPS = 2 * K * M * S * (G + 1)

F32 = mybir.dt.float32
BF16 = mybir.dt.bfloat16
I32 = mybir.dt.int32
U32 = mybir.dt.uint32
U16 = mybir.dt.uint16
U8 = mybir.dt.uint8
FP8X4 = mybir.dt.float8_e4m3fn_x4
FP4X4 = mybir.dt.float4_e2m1fn_x4
ALU = mybir.AluOpType
ACT = mybir.ActivationFunctionType

P = 128
PACK = 4
HALVES = M // P
PER_COL = 16
NODES = 128
CHUNKS = S // NODES
LAST = CHUNKS - 1


def tile_list_edge_silu_kernel(tc, xT, c, w4_words, w4_scales, w8_words, w8_scales, b, offs, out):
    nc = tc.nc
    with ExitStack() as ctx:
        keep = ctx.enter_context(tc.tile_pool(name="keep", bufs=1))
        psum = ctx.enter_context(tc.psum_pool(name="psum", bufs=1))

        offsets = keep.tile([P, G * S // PER_COL], U16, name="offsets")
        planes = [keep.tile([P, T], F32, name="plane%d" % t) for t in range(PACK)]
        c_raw = keep.tile([P, PACK, S], F32, name="c_raw")
        w4 = keep.tile([P, 2 * M], U8, name="w4", align_bytes=64)
        w4_sc = keep.tile([P, M], U8, name="w4_sc", align_bytes=64)
        w8 = keep.tile([P, M], U32, name="w8", align_bytes=64)
        w8_sc = keep.tile([P, M], U8, name="w8_sc", align_bytes=64)
        bias_rows = keep.tile([P, P], F32, name="bias_rows")
        bias = keep.tile([P, HALVES], F32, name="bias")
        warm = keep.tile([P, 2], F32, name="warm")
        ident = keep.tile([P, P], F32, name="ident")

        x_rows = xT.rearrange("(p t) n -> t p n", t=PACK)
        c_rows = c.rearrange("(p t) j -> p t j", t=PACK)
        out_rows = out.rearrange("(h p) j -> p h j", p=P)

        def load_scales(queue, tile, src):
            for q in range(4):
                queue.dma_start(tile[32 * q : 32 * q + 4, :].bitcast(I32), src[0, 4 * q : 4 * q + 4, :].bitcast(I32))

        nc.vector.memset(w8_sc[:].bitcast(U32), 0)
        nc.vector.memset(w4_sc[:].bitcast(U32), 0)
        nc.vector.memset(warm[:, 0:1], 0.0)
        nc.scalar.activation(warm[:, 1:2], warm[:, 0:1], ACT.Silu)
        nc.gpsimd.memset(bias_rows[:], 0.0)
        nc.gpsimd.dma_start(bias_rows[0:HALVES, :], b.rearrange("(h p) -> h p", p=P))
        make_identity(nc, ident[:])

        nc.sync.dma_start(c_raw[:], c_rows)
        nc.sync.dma_start(planes[0][:], x_rows[0])
        nc.sync.dma_start(offsets[:], offs)
        load_scales(nc.sync, w8_sc, w8_scales)
        nc.sync.dma_start(w8[:].bitcast(I32), w8_words[0].rearrange("p n t -> p (n t)").bitcast(I32))
        for t in range(1, PACK):
            nc.sync.dma_start(planes[t][:], x_rows[t])
        nc.sync.dma_start(w4[:].bitcast(I32), w4_words[0].bitcast(I32))
        load_scales(nc.sync, w4_sc, w4_scales)

        def quantize(name, src, n):
            codes = keep.tile([P, n], U32, name=name + "_codes", align_bytes=64)
            scales = keep.tile([P, n], U8, name=name + "_scales", align_bytes=64)
            nc.vector.quantize_mx(out=codes[:].bitcast(FP8X4), scales=scales[:], in_=src.rearrange("p j t -> p (j t)"))
            return codes, scales

        half = S // 2
        c_woven = [keep.tile([P, half, PACK], BF16, name="c_woven%d" % i, align_bytes=64) for i in range(2)]
        for i, copy in enumerate((nc.scalar.copy, nc.vector.tensor_copy)):
            copy(
                c_woven[i][:].rearrange("p (a i) t -> p a t i", i=4),
                c_raw[:, :, i * half : (i + 1) * half].rearrange("p t (a i) -> p a t i", i=4),
            )
        bias_acc = psum.tile([P, P], F32, name="bias_acc", tag="bank0")
        nc.tensor.transpose(bias_acc[:], bias_rows[:], ident[:])
        nc.vector.tensor_copy(bias[:], bias_acc[:, 0:HALVES])

        own = keep.tile([P, HALVES, S], F32, name="own")
        for i in range(2):
            codes, scales = quantize("c%d" % i, c_woven[i][:], half)
            own_acc = psum.tile([P, HALVES, half], F32, name="own_acc%d" % i, tag="bank%d" % (6 + i))
            for h in range(HALVES):
                nc.tensor.matmul_mx(
                    out=own_acc[:, h, :],
                    lhsT=w8[:, h * P : (h + 1) * P].bitcast(FP8X4),
                    lhsT_scale=w8_sc[:, h * P : (h + 1) * P],
                    rhs=codes[:].bitcast(FP8X4),
                    rhs_scale=scales[:],
                    start=True,
                    stop=True,
                )
            for h in range(HALVES):
                nc.scalar.activation(own[:, h, i * half : (i + 1) * half], own_acc[:, h, :], ACT.Identity, bias=bias[:, h : h + 1])

        diff = [[keep.tile([P, 2, S], F32, name="diff%d_%d" % (g, u)) for u in range(2)] for g in range(G)]
        woven = [keep.tile([P, S, PACK], BF16, name="woven%d" % g, align_bytes=64) for g in range(G)]

        def gather(g, t, j0, n):
            cols = slice((g * S + j0) // PER_COL, (g * S + j0 + n) // PER_COL)
            nc.vector.tensor_tensor(
                diff[g][t // 2][:, t % 2, j0 : j0 + n],
                planes[t][:].indirect(offsets[:, cols]),
                c_raw[:, t, j0 : j0 + n],
                ALU.subtract,
            )

        def weave(copy, g, u, j0, n):
            copy(woven[g][:, j0 : j0 + n, 2 * u : 2 * u + 2], diff[g][u][:, :, j0 : j0 + n].rearrange("p t j -> p j t"))

        for g in range(G):
            gather(g, 0, 0, S)
        for g in range(G):
            gather(g, 1, 0, S)
            weave(nc.scalar.copy, g, 0, 0, S)
        for g in range(G):
            gather(g, 2, 0, S)

        products, firsts, bests = {}, {}, {}

        def bring(k):
            for g in range(G):
                gather(g, 3, k * NODES, NODES)
                weave(nc.vector.tensor_copy if (g, k) in ((1, LAST),) else nc.scalar.copy, g, 1, k * NODES, NODES)

        def project(g, k):
            codes, scales = quantize("d%d_%d" % (g, k), woven[g][:, k * NODES : (k + 1) * NODES, :], NODES)
            acc = psum.tile([P, HALVES, NODES], F32, name="acc%d_%d" % (g, k), tag="bank%d" % (G * k + g))
            for h in range(HALVES):
                nc.tensor.matmul_mx(
                    out=acc[:, h, :],
                    lhsT=w4[:, 2 * h * P : 2 * (h + 1) * P].bitcast(FP4X4),
                    lhsT_scale=w4_sc[:, h * P : (h + 1) * P],
                    rhs=codes[:].bitcast(FP8X4),
                    rhs_scale=scales[:],
                    start=True,
                    stop=True,
                )
            products[g, k] = acc
            if g == 0:
                firsts[k] = keep.tile([P, HALVES, NODES], F32, name="first%d" % k)
                nc.scalar.copy(firsts[k][:], acc[:])

        def choose(k):
            bests[k] = keep.tile([P, HALVES, NODES], F32, name="best%d" % k)
            nc.vector.tensor_tensor(bests[k][:], products[1, k][:], firsts[k][:], ALU.max)

        def finish(k):
            j0 = k * NODES
            total = keep.tile([P, HALVES, NODES], F32, name="total%d" % k)
            nc.vector.tensor_tensor(total[:], bests[k][:], own[:, :, j0 : j0 + NODES], ALU.add)
            result = keep.tile([P, HALVES, NODES], F32, name="result%d" % k)
            nc.scalar.activation(result[:], total[:], ACT.Silu)
            nc.sync.dma_start(out_rows[:, :, j0 : j0 + NODES], result[:])

        for k in range(CHUNKS):
            bring(k)
            for g in range(G):
                project(g, k)
        choose(0)
        for k in range(CHUNKS):
            if k < LAST:
                choose(k + 1)
            finish(k)
